import numpy as np
import ml_dtypes


def mxq(x, axis, fmt="e4m3"):
    dtype, down = {"e4m3": (ml_dtypes.float8_e4m3fn, 7), "e5m2": (ml_dtypes.float8_e5m2, 14)}[fmt]
    v = np.moveaxis(np.asarray(x, np.float32).astype(ml_dtypes.bfloat16).astype(np.float64), axis, -1)
    blocks = v.reshape(v.shape[:-1] + (-1, 32))
    amax = np.abs(blocks).max(-1, keepdims=True)
    byte = np.maximum(np.where(amax > 0, np.frexp(amax)[1] - 1 + 127, 0) - down, 1)
    scale = np.exp2(byte - 127.0)
    codes = (blocks / scale).astype(np.float32).astype(dtype).astype(np.float64)
    return np.moveaxis((codes * scale).reshape(v.shape), -1, axis)


WIDE = False


def mx_kscale(k):
    if not WIDE:
        return np.ones(k)
    levels = np.array([10, -10, 5, -5, 0])
    if k % 512:
        return np.exp2(np.random.permutation(np.resize(levels, k // 32))).repeat(32)
    a = np.empty((k // 512, 16))
    for p in range(k // 512):
        a[p, :8] = np.random.permutation(np.resize(levels, 8))
        for g in range(8):
            far = levels[np.abs(levels - a[p, g]) >= 10]
            a[p, g + 8] = far[np.random.randint(len(far))]
    return np.exp2(a.ravel()).repeat(32)


def f64(x):
    return np.asarray(x).astype(np.float64)


def striped(idx):
    return np.tile(np.asarray(idx).reshape(-1, 16).T, (8, 1)).astype(np.uint16)


def unstriped(offs):
    return offs[:16].T.reshape(-1).astype(np.int64)


E2M1 = np.array([0.0, 0.5, 1.0, 1.5, 2.0, 3.0, 4.0, 6.0, -0.0, -0.5, -1.0, -1.5, -2.0, -3.0, -4.0, -6.0])


def pack_weight(w, fmt):
    k, n = w.shape
    w = f64(np.asarray(w, np.float32).astype(ml_dtypes.bfloat16)).reshape(k // 32, 32, n)
    amax = np.abs(w).max(1)
    if fmt == "e4m3":
        byte = np.frexp(amax)[1] - 1 + 127 - 7
    else:
        mant, ex = np.frexp(amax / 6.0)
        byte = np.where(mant > 0.5, ex, ex - 1) + 127
    byte = np.clip(np.where(amax > 0, byte, 1), 1, 254)
    scaled = (w * np.exp2(127.0 - byte)[:, None, :]).reshape(k, n).astype(np.float32)
    by_word = np.ascontiguousarray(scaled.reshape(k // 512, 128, 4, n).transpose(0, 1, 3, 2))
    if fmt == "e4m3":
        words = by_word.astype(ml_dtypes.float8_e4m3fn).view(np.uint8)
    else:
        c = by_word.astype(ml_dtypes.float4_e2m1fn).view(np.uint8) & 0xF
        words = (c[..., 0::2] | (c[..., 1::2] << 4)).reshape(k // 512, 128, 2 * n)
    return np.ascontiguousarray(words), np.ascontiguousarray(byte.astype(np.uint8).reshape(k // 512, 16, n))


def unpack_weight(words, scales, fmt):
    g, _, n = scales.shape
    words = np.ascontiguousarray(words).reshape(g, 128, n, -1)
    if fmt == "e4m3":
        vals = words.view(ml_dtypes.float8_e4m3fn).astype(np.float64)
    else:
        nib = np.empty((g, 128, n, 4), np.uint8)
        nib[..., 0::2] = words & 0xF
        nib[..., 1::2] = words >> 4
        vals = E2M1[nib]
    vals = vals * np.repeat(np.exp2(scales.astype(np.float64) - 127.0), 8, axis=1)[..., None]
    return vals.transpose(0, 1, 3, 2).reshape(g * 512, n)


def bf(x):
    return np.asarray(x, np.float32).astype(ml_dtypes.bfloat16)


def planes(Y):
    r, m = Y.shape
    b = f64(bf(Y)).reshape(r // 32, 32, m)
    amax = np.abs(b).max(1)
    byte = np.clip(np.where(amax > 0, np.frexp(amax)[1] - 1 + 127 - 7, 1), 1, 254)
    codes = (b * np.exp2(127.0 - byte)[:, None, :]).reshape(r, m).astype(np.float32).astype(ml_dtypes.float8_e4m3fn).view(np.uint8)
    words = codes.reshape(r // 512, 128, 4, m).transpose(0, 1, 3, 2)
    return np.ascontiguousarray(words), np.ascontiguousarray(byte.astype(np.uint8).reshape(r // 512, 16, m))


D, T, I, J, U, E = 512, 2048, 512, 512, 1024, 512


def setup_inputs():
    n = np.random.standard_normal
    idx = np.random.permutation(T)[:I]
    idx2 = np.random.permutation(U)[:J]
    idx3 = np.random.permutation(U)[:J]
    idx4 = np.random.permutation(U)[:J]
    fd = mx_kscale(D)
    fi = mx_kscale(I)
    ti = np.ones(T)
    ti[idx] = fi
    keysp = pack_weight(n((D, T)) / fd[:, None], "e2m1")
    return {
        "keys_words": keysp[0],
        "keys_scales": keysp[1],
        "notes": (n((D, U)) * 1.0 / np.sqrt(D) * fd[:, None]).astype(np.float32),
        "rowf": (np.random.uniform(0.02, 0.08, (I, 1)) * fi[:, None]).astype(np.float32),
        "vals": (n((E, T)) / ti).astype(np.float32),
        "offs": striped(idx),
        "offs2": striped(idx2),
        "offs3": striped(idx3),
        "offs4": striped(idx4),
    }


def reference(keys_words, keys_scales, notes, rowf, vals, offs, offs2, offs3, offs4):
    idx = unstriped(offs)
    idx2 = unstriped(offs2)
    idx3 = unstriped(offs3)
    idx4 = unstriped(offs4)
    keysu = unpack_weight(keys_words, keys_scales, "e2m1")
    keysidxg = keysu[:, idx]
    notesq = mxq(f64(notes), 0, "e4m3")
    g1 = keysidxg.T @ notesq
    lo2 = np.minimum(g1[:, idx2], g1[:, idx3])
    hi2 = np.maximum(g1[:, idx2], g1[:, idx3])
    g0 = np.maximum(lo2, np.minimum(hi2, g1[:, idx4]))
    gr1 = g0 * f64(rowf)
    vt1 = f64(vals)[:, idx].T
    vt1q = mxq(vt1, 0, "e4m3")
    gr1q = mxq(gr1, 0, "e4m3")
    o = vt1q.T @ gr1q
    words, scales = planes(o)
    return o, words, scales

@@ -1,0 +1,202 @@
+from contextlib import ExitStack
+
+import concourse.mybir as mybir
+from concourse.masks import make_identity
+
+D, T, I, J, U, E = 512, 2048, 512, 512, 1024, 512
+FLOPS = 2 * D * I * U + 2 * I * E * J
+
+F32 = mybir.dt.float32
+BF16 = mybir.dt.bfloat16
+I32 = mybir.dt.int32
+U32 = mybir.dt.uint32
+U16 = mybir.dt.uint16
+U8 = mybir.dt.uint8
+FP8X4 = mybir.dt.float8_e4m3fn_x4
+FP4X4 = mybir.dt.float4_e2m1fn_x4
+COPY = mybir.ActivationFunctionType.Copy
+MULT, MIN, MAX = mybir.AluOpType.mult, mybir.AluOpType.min, mybir.AluOpType.max
+
+P = 128
+PACK = 4
+BANK = 512
+NOTE_W = 256
+UNIT = 128
+CHUNKS = [(0, 384), (384, 128)]
+
+
+def weave_views(dst, src):
+    return (
+        dst.rearrange("p (c i) t -> p c t i", i=4),
+        src.rearrange("p t (c i) -> p c t i", i=4),
+    )
+
+
+def tile_attend_tab_middleof3_exchange_pl_kernel(
+    tc, keys_words, keys_scales, notes, rowf, vals, offs, offs2, offs3, offs4, out_0, out_1, out_2
+):
+    nc = tc.nc
+    with ExitStack() as ctx:
+        keep = ctx.enter_context(tc.tile_pool(name="keep", bufs=1))
+        psum = ctx.enter_context(tc.psum_pool(name="psum", bufs=8))
+
+        key_scales = keep.tile([P, T], U8, name="key_scales")
+        nc.gpsimd.memset(key_scales[:].bitcast(I32), 0)
+        token_list = keep.tile([P, I // 16], U16, name="token_list")
+        nc.sync.dma_start(token_list[:], offs)
+        for q in range(4):
+            nc.sync.dma_start(
+                key_scales[32 * q : 32 * q + 4, :].bitcast(I32), keys_scales[0, 4 * q : 4 * q + 4, :].bitcast(I32)
+            )
+        key_words = keep.tile([P, T], U16, name="key_words")
+        nc.sync.dma_start(key_words[:].bitcast(I32), keys_words[0].bitcast(I32))
+        notes_rows = notes.rearrange("(p t) u -> p t u", t=PACK)
+        notes_raw = []
+        for n in range(U // NOTE_W):
+            raw = keep.tile([P, PACK, NOTE_W], F32, name=f"notes_raw{n}")
+            nc.sync.dma_start(raw[:], notes_rows[:, :, n * NOTE_W : (n + 1) * NOTE_W])
+            notes_raw.append(raw)
+        column_lists = []
+        for n, src in enumerate((offs2, offs3, offs4)):
+            lst = keep.tile([P, J // 16], U16, name=f"column_list{n}")
+            nc.sync.dma_start(lst[:], src)
+            column_lists.append(lst)
+        factor = keep.tile([P, PACK], F32, name="factor")
+        nc.sync.dma_start(factor[:], rowf.rearrange("(p r) o -> p (r o)", r=PACK))
+        vals_rows = vals.rearrange("(p t) c -> t p c", t=PACK)
+        vals_raw = []
+        for t in range(PACK):
+            raw = keep.tile([P, T], F32, name=f"vals_raw{t}", tag=f"vals_raw{t}")
+            nc.sync.dma_start(raw[:], vals_rows[t])
+            vals_raw.append(raw)
+        identity = keep.tile([P, P], F32, name="identity")
+        make_identity(nc, identity[:])
+
+        dealt_scales = keep.tile([P, PACK, P], U8, name="dealt_scales", align_bytes=64)
+        nc.vector.tensor_copy(dealt_scales[:].rearrange("p r s -> p s r"), key_scales[:].indirect(token_list[:]))
+        picked_words = keep.tile([P, I], U16, name="picked_words")
+        nc.vector.tensor_copy(picked_words[:], key_words[:].indirect(token_list[:]))
+        dealt_words = keep.tile([P, PACK, P], U16, name="dealt_words", align_bytes=64)
+        nc.vector.tensor_copy(dealt_words[:], picked_words[:].rearrange("p (s r) -> p r s", r=PACK))
+
+        g1 = [keep.tile([P, U], F32, name=f"g1_{r}") for r in range(PACK)]
+        per_bank = BANK // NOTE_W
+        for h in range(U // BANK):
+            banks = [psum.tile([P, BANK], F32, name=f"g1_bank{h}_{r}", tag="bank") for r in range(PACK)]
+            for k in range(per_bank):
+                n = h * per_bank + k
+                woven = keep.tile([P, NOTE_W, PACK], BF16, name=f"notes_woven{n}", align_bytes=64)
+                dst, src = weave_views(woven[:], notes_raw[n][:])
+                if h == 0:
+                    nc.scalar.activation(dst, src, COPY)
+                else:
+                    nc.vector.tensor_copy(dst, src)
+                codes = keep.tile([P, NOTE_W], U32, name=f"notes_codes{n}", align_bytes=64)
+                scales = keep.tile([P, NOTE_W], U8, name=f"notes_scales{n}", align_bytes=64)
+                nc.vector.quantize_mx(codes[:].bitcast(FP8X4), scales[:], woven[:].rearrange("p u t -> p (u t)"))
+                for r in range(PACK):
+                    nc.tensor.matmul_mx(
+                        banks[r][:, k * NOTE_W : (k + 1) * NOTE_W],
+                        lhsT=dealt_words[:, r, :].bitcast(FP4X4),
+                        lhsT_scale=dealt_scales[:, r, :],
+                        rhs=codes[:].bitcast(FP8X4),
+                        rhs_scale=scales[:],
+                        start=True,
+                        stop=True,
+                    )
+            for r in range(PACK):
+                if h == 1 and r == 0:
+                    nc.vector.tensor_copy(g1[r][:, h * BANK : (h + 1) * BANK], banks[r][:])
+                else:
+                    nc.scalar.copy(g1[r][:, h * BANK : (h + 1) * BANK], banks[r][:])
+
+        val_codes = keep.tile([P, E], U32, name="val_codes", align_bytes=64)
+        val_scales = keep.tile([P, E], U8, name="val_scales", align_bytes=64)
+
+        def values(t):
+            picked = keep.tile([P, I], BF16, name=f"picked_vals{t}")
+            nc.scalar.activation(picked[:], vals_raw[t][:].indirect(token_list[:]), COPY)
+            pairs = picked[:].bitcast(F32)
+            turned = psum.tile([P, 2, P], F32, name=f"turned{t}", tag="bank")
+            for u in range(2):
+                nc.tensor.transpose(turned[:, u, :], pairs[:, u : I // 2 : 2], identity[:])
+            woven = keep.tile([P, P * PACK], BF16, name=f"vals_woven{t}", align_bytes=64)
+            nc.scalar.copy(
+                woven[:].bitcast(F32).rearrange("p (e u) -> p e u", u=2), turned[:].rearrange("p u e -> p e u")
+            )
+            cols = slice(t * P, (t + 1) * P)
+            nc.vector.quantize_mx(val_codes[:, cols].bitcast(FP8X4), val_scales[:, cols], woven[:])
+
+        out_codes = keep.tile([P, J], U32, name="out_codes", align_bytes=64)
+        out_scales = keep.tile([P, J], U8, name="out_scales", align_bytes=64)
+        out_rows = out_0.rearrange("(p t) j -> p t j", t=PACK)
+        code_rows = out_1[0].rearrange("p c r -> p (c r)").bitcast(I32)
+
+        def table(c, j0, w):
+            a, bf, lo, hi, mid = [keep.tile([P, PACK, w], F32, name=f"{nm}{c}") for nm in ("a", "bf", "lo", "hi", "mid")]
+            lists = [lst[:, j0 // 16 : (j0 + w) // 16] for lst in column_lists]
+            if c > 0:
+                later = keep.tile([P, PACK, 2, w], F32, name=f"later{c}", tag=f"vals_raw{(PACK - 2 + c) % PACK}")
+            for r in range(PACK):
+                f = factor[:, r : r + 1]
+                if c > 0:
+                    pair = later[:, r]
+                elif r > 0:
+                    pair = keep.tile([P, 2, w], F32, name=f"pair{r}", tag=f"vals_raw{r - 1}")[:]
+                else:
+                    pair = keep.tile([P, 2, w], F32, name="pair0")[:]
+                b, third = pair[:, 0, :], pair[:, 1, :]
+                nc.scalar.activation(b, g1[r][:].indirect(lists[1]), COPY)
+                nc.vector.tensor_copy(a[:, r, :], g1[r][:].indirect(lists[0]))
+                nc.scalar.activation(third, g1[r][:].indirect(lists[2]), COPY)
+                nc.vector.tensor_scalar(bf[:, r, :], b, f, None, MULT)
+                nc.vector.scalar_tensor_tensor(hi[:, r, :], a[:, r, :], f, bf[:, r, :], MULT, MAX)
+                nc.vector.scalar_tensor_tensor(lo[:, r, :], a[:, r, :], f, bf[:, r, :], MULT, MIN)
+                nc.vector.scalar_tensor_tensor(mid[:, r, :], third, f, hi[:, r, :], MULT, MIN)
+                if c == 0:
+                    values(r)
+            return lo, mid
+
+        def product(lo, mid, j0, k):
+            cols = slice(k * UNIT, (k + 1) * UNIT)
+            jcols = slice(j0 + k * UNIT, j0 + (k + 1) * UNIT)
+            woven = keep.tile([P, UNIT, PACK], BF16, name=f"gr1_woven{jcols.start}", align_bytes=64)
+            dst, lo_view = weave_views(woven[:], lo[:, :, cols])
+            mid_view = weave_views(woven[:], mid[:, :, cols])[1]
+            nc.vector.tensor_tensor(dst, lo_view, mid_view, MAX)
+            codes = keep.tile([P, UNIT], U32, name=f"gr1_codes{jcols.start}", align_bytes=64)
+            scales = keep.tile([P, UNIT], U8, name=f"gr1_scales{jcols.start}", align_bytes=64)
+            nc.vector.quantize_mx(codes[:].bitcast(FP8X4), scales[:], woven[:].rearrange("p j r -> p (j r)"))
+            bank = psum.tile([P, PACK, UNIT], F32, name=f"out_bank{jcols.start}", tag="bank")
+            for t in range(PACK):
+                ecols = slice(t * P, (t + 1) * P)
+                nc.tensor.matmul_mx(
+                    bank[:, t, :],
+                    lhsT=val_codes[:, ecols].bitcast(FP8X4),
+                    lhsT_scale=val_scales[:, ecols],
+                    rhs=codes[:].bitcast(FP8X4),
+                    rhs_scale=scales[:],
+                    start=True,
+                    stop=True,
+                )
+            result = keep.tile([P, PACK, UNIT], F32, name=f"result{jcols.start}")
+            nc.scalar.copy(result[:], bank[:])
+            nc.sync.dma_start(out_rows[:, :, jcols], result[:])
+            rounded = keep.tile([P, UNIT, PACK], BF16, name=f"rounded{jcols.start}", align_bytes=64)
+            dst, src = weave_views(rounded[:], result[:])
+            nc.vector.tensor_copy(dst, src)
+            nc.vector.quantize_mx(
+                out_codes[:, jcols].bitcast(FP8X4), out_scales[:, jcols], rounded[:].rearrange("p j t -> p (j t)")
+            )
+            nc.sync.dma_start(code_rows[:, jcols], out_codes[:, jcols].bitcast(I32))
+
+        for c, (j0, w) in enumerate(CHUNKS):
+            lo, mid = table(c, j0, w)
+            for k in range(w // UNIT):
+                product(lo, mid, j0, k)
+
+        for q in range(4):
+            queue = nc.scalar if q % 2 else nc.sync
+            queue.dma_start(
+                out_2[0, 4 * q : 4 * q + 4, :].bitcast(I32), out_scales[32 * q : 32 * q + 4, :].bitcast(I32)
+            )

@@ -38,29 +38,30 @@ def tile_attend_tab_middleof3_exchange_pl_kernel(
     nc = tc.nc
     with ExitStack() as ctx:
         keep = ctx.enter_context(tc.tile_pool(name="keep", bufs=1))
-        psum = ctx.enter_context(tc.psum_pool(name="psum", bufs=8))
+        psum = ctx.enter_context(tc.psum_pool(name="psum", bufs=4))
+        g1_psum = ctx.enter_context(tc.psum_pool(name="g1_psum", bufs=1))
 
-        key_scales = keep.tile([P, T], U8, name="key_scales")
-        nc.gpsimd.memset(key_scales[:].bitcast(I32), 0)
         token_list = keep.tile([P, I // 16], U16, name="token_list")
         nc.sync.dma_start(token_list[:], offs)
+        scale_rows = keep.tile([P, T], U8, name="scale_rows")
+        key_scales = keep.tile([P, T], U8, name="key_scales")
+        nc.vector.memset(key_scales[:].bitcast(I32), 0)
         for q in range(4):
-            nc.sync.dma_start(
-                key_scales[32 * q : 32 * q + 4, :].bitcast(I32), keys_scales[0, 4 * q : 4 * q + 4, :].bitcast(I32)
-            )
+            live = slice(32 * q, 32 * q + 4)
+            nc.sync.dma_start(scale_rows[live, :].bitcast(I32), keys_scales[0, 4 * q : 4 * q + 4, :].bitcast(I32))
+            nc.vector.tensor_copy(key_scales[live, :].bitcast(I32), scale_rows[live, :].bitcast(I32))
         key_words = keep.tile([P, T], U16, name="key_words")
         nc.sync.dma_start(key_words[:].bitcast(I32), keys_words[0].bitcast(I32))
         notes_rows = notes.rearrange("(p t) u -> p t u", t=PACK)
         notes_raw = []
         for n in range(U // NOTE_W):
-            raw = keep.tile([P, PACK, NOTE_W], F32, name=f"notes_raw{n}")
+            raw = keep.tile([P, PACK, NOTE_W], F32, name=f"notes_raw{n}", tag=f"notes_raw{n}")
             nc.sync.dma_start(raw[:], notes_rows[:, :, n * NOTE_W : (n + 1) * NOTE_W])
             notes_raw.append(raw)
-        column_lists = []
-        for n, src in enumerate((offs2, offs3, offs4)):
-            lst = keep.tile([P, J // 16], U16, name=f"column_list{n}")
-            nc.sync.dma_start(lst[:], src)
-            column_lists.append(lst)
+        column_lists = [keep.tile([P, J // 16], U16, name=f"column_list{n}") for n in range(3)]
+        nc.sync.dma_start(column_lists[0][:], offs2)
+        nc.sync.dma_start(column_lists[1][:], offs3)
+        nc.sync.dma_start(column_lists[2][:], offs4)
         factor = keep.tile([P, PACK], F32, name="factor")
         nc.sync.dma_start(factor[:], rowf.rearrange("(p r) o -> p (r o)", r=PACK))
         vals_rows = vals.rearrange("(p t) c -> t p c", t=PACK)
@@ -79,24 +80,29 @@ def tile_attend_tab_middleof3_exchange_pl_kernel(
         dealt_words = keep.tile([P, PACK, P], U16, name="dealt_words", align_bytes=64)
         nc.vector.tensor_copy(dealt_words[:], picked_words[:].rearrange("p (s r) -> p r s", r=PACK))
 
-        g1 = [keep.tile([P, U], F32, name=f"g1_{r}") for r in range(PACK)]
+        g1 = [keep.tile([P, U], F32, name=f"g1_{r}", tag=f"notes_raw{(r + 2) % PACK}") for r in range(PACK)]
         per_bank = BANK // NOTE_W
-        for h in range(U // BANK):
-            banks = [psum.tile([P, BANK], F32, name=f"g1_bank{h}_{r}", tag="bank") for r in range(PACK)]
-            for k in range(per_bank):
-                n = h * per_bank + k
-                woven = keep.tile([P, NOTE_W, PACK], BF16, name=f"notes_woven{n}", align_bytes=64)
-                dst, src = weave_views(woven[:], notes_raw[n][:])
-                if h == 0:
-                    nc.scalar.activation(dst, src, COPY)
-                else:
-                    nc.vector.tensor_copy(dst, src)
-                codes = keep.tile([P, NOTE_W], U32, name=f"notes_codes{n}", align_bytes=64)
-                scales = keep.tile([P, NOTE_W], U8, name=f"notes_scales{n}", align_bytes=64)
-                nc.vector.quantize_mx(codes[:].bitcast(FP8X4), scales[:], woven[:].rearrange("p u t -> p (u t)"))
-                for r in range(PACK):
+        note_operands = []
+        for n in range(U // NOTE_W):
+            woven = keep.tile([P, NOTE_W, PACK], BF16, name=f"notes_woven{n}", tag=f"notes_woven{n if n < 3 else 1}", align_bytes=64)
+            dst, src = weave_views(woven[:], notes_raw[n][:])
+            if n < 3:
+                nc.scalar.activation(dst, src, COPY)
+            else:
+                nc.vector.tensor_copy(dst, src)
+            codes = keep.tile([P, NOTE_W], U32, name=f"notes_codes{n}", align_bytes=64)
+            scales = keep.tile([P, NOTE_W], U8, name=f"notes_scales{n}", align_bytes=64)
+            nc.vector.quantize_mx(codes[:].bitcast(FP8X4), scales[:], woven[:].rearrange("p u t -> p (u t)"))
+            note_operands.append((codes, scales))
+        for r in range(PACK):
+            for h in range(U // BANK):
+                early = r < 2 and h == 0
+                tag = f"early{r}" if early else f"late{r if r < 2 else h}"
+                bank = g1_psum.tile([P, BANK], F32, name=f"g1_bank{r}_{h}", tag=tag)[:]
+                for k in range(per_bank):
+                    codes, scales = note_operands[h * per_bank + k]
                     nc.tensor.matmul_mx(
-                        banks[r][:, k * NOTE_W : (k + 1) * NOTE_W],
+                        bank[:, k * NOTE_W : (k + 1) * NOTE_W],
                         lhsT=dealt_words[:, r, :].bitcast(FP4X4),
                         lhsT_scale=dealt_scales[:, r, :],
                         rhs=codes[:].bitcast(FP8X4),
@@ -104,69 +110,69 @@ def tile_attend_tab_middleof3_exchange_pl_kernel(
                         start=True,
                         stop=True,
                     )
-            for r in range(PACK):
                 if h == 1 and r == 0:
-                    nc.vector.tensor_copy(g1[r][:, h * BANK : (h + 1) * BANK], banks[r][:])
+                    nc.vector.tensor_copy(g1[r][:, h * BANK : (h + 1) * BANK], bank)
                 else:
-                    nc.scalar.copy(g1[r][:, h * BANK : (h + 1) * BANK], banks[r][:])
-
-        val_codes = keep.tile([P, E], U32, name="val_codes", align_bytes=64)
-        val_scales = keep.tile([P, E], U8, name="val_scales", align_bytes=64)
-
-        def values(t):
-            picked = keep.tile([P, I], BF16, name=f"picked_vals{t}")
-            nc.scalar.activation(picked[:], vals_raw[t][:].indirect(token_list[:]), COPY)
-            pairs = picked[:].bitcast(F32)
-            turned = psum.tile([P, 2, P], F32, name=f"turned{t}", tag="bank")
-            for u in range(2):
-                nc.tensor.transpose(turned[:, u, :], pairs[:, u : I // 2 : 2], identity[:])
-            woven = keep.tile([P, P * PACK], BF16, name=f"vals_woven{t}", align_bytes=64)
-            nc.scalar.copy(
-                woven[:].bitcast(F32).rearrange("p (e u) -> p e u", u=2), turned[:].rearrange("p u e -> p e u")
-            )
-            cols = slice(t * P, (t + 1) * P)
-            nc.vector.quantize_mx(val_codes[:, cols].bitcast(FP8X4), val_scales[:, cols], woven[:])
+                    nc.scalar.copy(g1[r][:, h * BANK : (h + 1) * BANK], bank)
 
         out_codes = keep.tile([P, J], U32, name="out_codes", align_bytes=64)
         out_scales = keep.tile([P, J], U8, name="out_scales", align_bytes=64)
         out_rows = out_0.rearrange("(p t) j -> p t j", t=PACK)
         code_rows = out_1[0].rearrange("p c r -> p (c r)").bitcast(I32)
 
-        def table(c, j0, w):
-            a, bf, lo, hi, mid = [keep.tile([P, PACK, w], F32, name=f"{nm}{c}") for nm in ("a", "bf", "lo", "hi", "mid")]
-            lists = [lst[:, j0 // 16 : (j0 + w) // 16] for lst in column_lists]
-            if c > 0:
-                later = keep.tile([P, PACK, 2, w], F32, name=f"later{c}", tag=f"vals_raw{(PACK - 2 + c) % PACK}")
-            for r in range(PACK):
-                f = factor[:, r : r + 1]
-                if c > 0:
-                    pair = later[:, r]
-                elif r > 0:
-                    pair = keep.tile([P, 2, w], F32, name=f"pair{r}", tag=f"vals_raw{r - 1}")[:]
-                else:
-                    pair = keep.tile([P, 2, w], F32, name="pair0")[:]
-                b, third = pair[:, 0, :], pair[:, 1, :]
-                nc.scalar.activation(b, g1[r][:].indirect(lists[1]), COPY)
-                nc.vector.tensor_copy(a[:, r, :], g1[r][:].indirect(lists[0]))
-                nc.scalar.activation(third, g1[r][:].indirect(lists[2]), COPY)
-                nc.vector.tensor_scalar(bf[:, r, :], b, f, None, MULT)
-                nc.vector.scalar_tensor_tensor(hi[:, r, :], a[:, r, :], f, bf[:, r, :], MULT, MAX)
-                nc.vector.scalar_tensor_tensor(lo[:, r, :], a[:, r, :], f, bf[:, r, :], MULT, MIN)
-                nc.vector.scalar_tensor_tensor(mid[:, r, :], third, f, hi[:, r, :], MULT, MIN)
-                if c == 0:
-                    values(r)
-            return lo, mid
+        a, bf, lo, mid = [keep.tile([P, PACK, J], F32, name=nm) for nm in ("a", "bf", "lo", "mid")]
+        hi = keep.tile([P, PACK, J], F32, name="hi", tag="hi", align_bytes=64)
+        for r in range(PACK):
+            f = factor[:, r : r + 1]
+            b = keep.tile([P, J], F32, name=f"b{r}", tag=f"b{r}")
+            third = keep.tile([P, J], F32, name=f"third{r}", tag=f"third{r}")
+            nc.vector.tensor_copy(a[:, r, :], g1[r][:].indirect(column_lists[0][:]))
+            if r < PACK - 1:
+                nc.scalar.activation(b[:], g1[r][:].indirect(column_lists[1][:]), COPY)
+                nc.scalar.activation(third[:], g1[r][:].indirect(column_lists[2][:]), COPY)
+            else:
+                nc.vector.tensor_copy(b[:], g1[r][:].indirect(column_lists[1][:]))
+                nc.vector.tensor_copy(third[:], g1[r][:].indirect(column_lists[2][:]))
+            nc.vector.tensor_scalar(bf[:, r, :], b[:], f, None, MULT)
+            nc.vector.scalar_tensor_tensor(hi[:, r, :], a[:, r, :], f, bf[:, r, :], MULT, MAX)
+            nc.vector.scalar_tensor_tensor(lo[:, r, :], a[:, r, :], f, bf[:, r, :], MULT, MIN)
+            nc.vector.scalar_tensor_tensor(mid[:, r, :], third[:], f, hi[:, r, :], MULT, MIN)
 
-        def product(lo, mid, j0, k):
+        vals_woven = keep.tile([P, PACK, P * PACK], BF16, name="vals_woven", align_bytes=64)
+        for t in range(PACK):
+            picked = keep.tile([P, I], BF16, name=f"picked_vals{t}", tag=("b0", "third0", "b1", "third1")[t])
+            nc.scalar.activation(picked[:], vals_raw[t][:].indirect(token_list[:]), COPY)
+            pairs = picked[:].bitcast(F32)
+            turned = psum.tile([P, 2, P], F32, name=f"turned{t}", tag="bank")
+            for u in range(2):
+                nc.tensor.transpose(turned[:, u, :], pairs[:, u : I // 2 : 2], identity[:])
+            nc.scalar.copy(
+                vals_woven[:, t, :].bitcast(F32).rearrange("p (e u) -> p e u", u=2),
+                turned[:].rearrange("p u e -> p e u"),
+            )
+
+        gr1_operands = []
+        for k in range(J // UNIT):
             cols = slice(k * UNIT, (k + 1) * UNIT)
-            jcols = slice(j0 + k * UNIT, j0 + (k + 1) * UNIT)
-            woven = keep.tile([P, UNIT, PACK], BF16, name=f"gr1_woven{jcols.start}", align_bytes=64)
+            woven = keep.tile([P, UNIT, PACK], BF16, name=f"gr1_woven{k}", align_bytes=64)
             dst, lo_view = weave_views(woven[:], lo[:, :, cols])
             mid_view = weave_views(woven[:], mid[:, :, cols])[1]
             nc.vector.tensor_tensor(dst, lo_view, mid_view, MAX)
-            codes = keep.tile([P, UNIT], U32, name=f"gr1_codes{jcols.start}", align_bytes=64)
-            scales = keep.tile([P, UNIT], U8, name=f"gr1_scales{jcols.start}", align_bytes=64)
+            codes = keep.tile([P, UNIT], U32, name=f"gr1_codes{k}", align_bytes=64)
+            scales = keep.tile([P, UNIT], U8, name=f"gr1_scales{k}", align_bytes=64)
             nc.vector.quantize_mx(codes[:].bitcast(FP8X4), scales[:], woven[:].rearrange("p j r -> p (j r)"))
+            gr1_operands.append((codes, scales))
+            if k == 0:
+                val_codes = keep.tile([P, E], U32, name="val_codes", tag="hi", align_bytes=64)
+                val_scales = keep.tile([P, E], U8, name="val_scales", align_bytes=64)
+                nc.vector.quantize_mx(
+                    val_codes[:].bitcast(FP8X4), val_scales[:], vals_woven[:].rearrange("p t x -> p (t x)")
+                )
+
+
+        def product(k):
+            jcols = slice(k * UNIT, (k + 1) * UNIT)
+            codes, scales = gr1_operands[k]
             bank = psum.tile([P, PACK, UNIT], F32, name=f"out_bank{jcols.start}", tag="bank")
             for t in range(PACK):
                 ecols = slice(t * P, (t + 1) * P)
@@ -190,10 +196,8 @@ def tile_attend_tab_middleof3_exchange_pl_kernel(
             )
             nc.sync.dma_start(code_rows[:, jcols], out_codes[:, jcols].bitcast(I32))
 
-        for c, (j0, w) in enumerate(CHUNKS):
-            lo, mid = table(c, j0, w)
-            for k in range(w // UNIT):
-                product(lo, mid, j0, k)
+        for k in range(J // UNIT):
+            product(k)
 
         for q in range(4):
             queue = nc.scalar if q % 2 else nc.sync

@@ -131,7 +131,8 @@ def tile_attend_tab_middleof3_exchange_pl_kernel(
                 nc.scalar.activation(b[:], g1[r][:].indirect(column_lists[1][:]), COPY)
                 nc.scalar.activation(third[:], g1[r][:].indirect(column_lists[2][:]), COPY)
             else:
-                nc.vector.tensor_copy(b[:], g1[r][:].indirect(column_lists[1][:]))
+                nc.scalar.activation(b[:, : J // 2], g1[r][:].indirect(column_lists[1][:, : J // 32]), COPY)
+                nc.vector.tensor_copy(b[:, J // 2 :], g1[r][:].indirect(column_lists[1][:, J // 32 :]))
                 nc.vector.tensor_copy(third[:], g1[r][:].indirect(column_lists[2][:]))
             nc.vector.tensor_scalar(bf[:, r, :], b[:], f, None, MULT)
             nc.vector.scalar_tensor_tensor(hi[:, r, :], a[:, r, :], f, bf[:, r, :], MULT, MAX)
@@ -154,7 +155,7 @@ def tile_attend_tab_middleof3_exchange_pl_kernel(
         gr1_operands = []
         for k in range(J // UNIT):
             cols = slice(k * UNIT, (k + 1) * UNIT)
-            woven = keep.tile([P, UNIT, PACK], BF16, name=f"gr1_woven{k}", align_bytes=64)
+            woven = keep.tile([P, UNIT, PACK], BF16, name=f"gr1_woven{k}", tag=f"unit_woven{k}", align_bytes=64)
             dst, lo_view = weave_views(woven[:], lo[:, :, cols])
             mid_view = weave_views(woven[:], mid[:, :, cols])[1]
             nc.vector.tensor_tensor(dst, lo_view, mid_view, MAX)
@@ -162,7 +163,7 @@ def tile_attend_tab_middleof3_exchange_pl_kernel(
             scales = keep.tile([P, UNIT], U8, name=f"gr1_scales{k}", align_bytes=64)
             nc.vector.quantize_mx(codes[:].bitcast(FP8X4), scales[:], woven[:].rearrange("p j r -> p (j r)"))
             gr1_operands.append((codes, scales))
-            if k == 0:
+            if k == 1:
                 val_codes = keep.tile([P, E], U32, name="val_codes", tag="hi", align_bytes=64)
                 val_scales = keep.tile([P, E], U8, name="val_scales", align_bytes=64)
                 nc.vector.quantize_mx(
@@ -188,7 +189,7 @@ def tile_attend_tab_middleof3_exchange_pl_kernel(
             result = keep.tile([P, PACK, UNIT], F32, name=f"result{jcols.start}")
             nc.scalar.copy(result[:], bank[:])
             nc.sync.dma_start(out_rows[:, :, jcols], result[:])
-            rounded = keep.tile([P, UNIT, PACK], BF16, name=f"rounded{jcols.start}", align_bytes=64)
+            rounded = keep.tile([P, UNIT, PACK], BF16, name=f"rounded{jcols.start}", tag=f"unit_woven{J // UNIT - 1 - k}", align_bytes=64)
             dst, src = weave_views(rounded[:], result[:])
             nc.vector.tensor_copy(dst, src)
             nc.vector.quantize_mx(

from contextlib import ExitStack

import concourse.mybir as mybir
from concourse.masks import make_identity

D, T, I, J, U, E = 512, 2048, 512, 512, 1024, 512
FLOPS = 2 * D * I * U + 2 * I * E * J

F32 = mybir.dt.float32
BF16 = mybir.dt.bfloat16
I32 = mybir.dt.int32
U32 = mybir.dt.uint32
U16 = mybir.dt.uint16
U8 = mybir.dt.uint8
FP8X4 = mybir.dt.float8_e4m3fn_x4
FP4X4 = mybir.dt.float4_e2m1fn_x4
COPY = mybir.ActivationFunctionType.Copy
MULT, MIN, MAX = mybir.AluOpType.mult, mybir.AluOpType.min, mybir.AluOpType.max

P = 128
PACK = 4
BANK = 512
NOTE_W = 256
UNIT = 128
CHUNKS = [(0, 384), (384, 128)]


def weave_views(dst, src):
    return (
        dst.rearrange("p (c i) t -> p c t i", i=4),
        src.rearrange("p t (c i) -> p c t i", i=4),
    )


def tile_attend_tab_middleof3_exchange_pl_kernel(
    tc, keys_words, keys_scales, notes, rowf, vals, offs, offs2, offs3, offs4, out_0, out_1, out_2
):
    nc = tc.nc
    with ExitStack() as ctx:
        keep = ctx.enter_context(tc.tile_pool(name="keep", bufs=1))
        psum = ctx.enter_context(tc.psum_pool(name="psum", bufs=4))
        g1_psum = ctx.enter_context(tc.psum_pool(name="g1_psum", bufs=1))

        token_list = keep.tile([P, I // 16], U16, name="token_list")
        nc.sync.dma_start(token_list[:], offs)
        scale_rows = keep.tile([P, T], U8, name="scale_rows")
        key_scales = keep.tile([P, T], U8, name="key_scales")
        nc.vector.memset(key_scales[:].bitcast(I32), 0)
        for q in range(4):
            live = slice(32 * q, 32 * q + 4)
            nc.sync.dma_start(scale_rows[live, :].bitcast(I32), keys_scales[0, 4 * q : 4 * q + 4, :].bitcast(I32))
            nc.vector.tensor_copy(key_scales[live, :].bitcast(I32), scale_rows[live, :].bitcast(I32))
        key_words = keep.tile([P, T], U16, name="key_words")
        nc.sync.dma_start(key_words[:].bitcast(I32), keys_words[0].bitcast(I32))
        notes_rows = notes.rearrange("(p t) u -> p t u", t=PACK)
        notes_raw = []
        for n in range(U // NOTE_W):
            raw = keep.tile([P, PACK, NOTE_W], F32, name=f"notes_raw{n}", tag=f"notes_raw{n}")
            nc.sync.dma_start(raw[:], notes_rows[:, :, n * NOTE_W : (n + 1) * NOTE_W])
            notes_raw.append(raw)
        column_lists = [keep.tile([P, J // 16], U16, name=f"column_list{n}") for n in range(3)]
        nc.sync.dma_start(column_lists[0][:], offs2)
        nc.sync.dma_start(column_lists[1][:], offs3)
        nc.sync.dma_start(column_lists[2][:], offs4)
        factor = keep.tile([P, PACK], F32, name="factor")
        nc.sync.dma_start(factor[:], rowf.rearrange("(p r) o -> p (r o)", r=PACK))
        vals_rows = vals.rearrange("(p t) c -> t p c", t=PACK)
        vals_raw = []
        for t in range(PACK):
            raw = keep.tile([P, T], F32, name=f"vals_raw{t}", tag=f"vals_raw{t}")
            nc.sync.dma_start(raw[:], vals_rows[t])
            vals_raw.append(raw)
        identity = keep.tile([P, P], F32, name="identity")
        make_identity(nc, identity[:])

        dealt_scales = keep.tile([P, PACK, P], U8, name="dealt_scales", align_bytes=64)
        nc.vector.tensor_copy(dealt_scales[:].rearrange("p r s -> p s r"), key_scales[:].indirect(token_list[:]))
        picked_words = keep.tile([P, I], U16, name="picked_words")
        nc.vector.tensor_copy(picked_words[:], key_words[:].indirect(token_list[:]))
        dealt_words = keep.tile([P, PACK, P], U16, name="dealt_words", align_bytes=64)
        nc.vector.tensor_copy(dealt_words[:], picked_words[:].rearrange("p (s r) -> p r s", r=PACK))

        g1 = [keep.tile([P, U], F32, name=f"g1_{r}", tag=f"notes_raw{(r + 2) % PACK}") for r in range(PACK)]
        per_bank = BANK // NOTE_W
        note_operands = []
        for n in range(U // NOTE_W):
            woven = keep.tile([P, NOTE_W, PACK], BF16, name=f"notes_woven{n}", tag=f"notes_woven{n if n < 3 else 1}", align_bytes=64)
            dst, src = weave_views(woven[:], notes_raw[n][:])
            if n < 3:
                nc.scalar.activation(dst, src, COPY)
            else:
                nc.vector.tensor_copy(dst, src)
            codes = keep.tile([P, NOTE_W], U32, name=f"notes_codes{n}", align_bytes=64)
            scales = keep.tile([P, NOTE_W], U8, name=f"notes_scales{n}", align_bytes=64)
            nc.vector.quantize_mx(codes[:].bitcast(FP8X4), scales[:], woven[:].rearrange("p u t -> p (u t)"))
            note_operands.append((codes, scales))
        for r in range(PACK):
            for h in range(U // BANK):
                early = r < 2 and h == 0
                tag = f"early{r}" if early else f"late{r if r < 2 else h}"
                bank = g1_psum.tile([P, BANK], F32, name=f"g1_bank{r}_{h}", tag=tag)[:]
                for k in range(per_bank):
                    codes, scales = note_operands[h * per_bank + k]
                    nc.tensor.matmul_mx(
                        bank[:, k * NOTE_W : (k + 1) * NOTE_W],
                        lhsT=dealt_words[:, r, :].bitcast(FP4X4),
                        lhsT_scale=dealt_scales[:, r, :],
                        rhs=codes[:].bitcast(FP8X4),
                        rhs_scale=scales[:],
                        start=True,
                        stop=True,
                    )
                if h == 1 and r == 0:
                    nc.vector.tensor_copy(g1[r][:, h * BANK : (h + 1) * BANK], bank)
                else:
                    nc.scalar.copy(g1[r][:, h * BANK : (h + 1) * BANK], bank)

        out_codes = keep.tile([P, J], U32, name="out_codes", align_bytes=64)
        out_scales = keep.tile([P, J], U8, name="out_scales", align_bytes=64)
        out_rows = out_0.rearrange("(p t) j -> p t j", t=PACK)
        code_rows = out_1[0].rearrange("p c r -> p (c r)").bitcast(I32)

        a, bf, lo, mid = [keep.tile([P, PACK, J], F32, name=nm) for nm in ("a", "bf", "lo", "mid")]
        hi = keep.tile([P, PACK, J], F32, name="hi", tag="hi", align_bytes=64)
        for r in range(PACK):
            f = factor[:, r : r + 1]
            b = keep.tile([P, J], F32, name=f"b{r}", tag=f"b{r}")
            third = keep.tile([P, J], F32, name=f"third{r}", tag=f"third{r}")
            nc.vector.tensor_copy(a[:, r, :], g1[r][:].indirect(column_lists[0][:]))
            if r < PACK - 1:
                nc.scalar.activation(b[:], g1[r][:].indirect(column_lists[1][:]), COPY)
                nc.scalar.activation(third[:], g1[r][:].indirect(column_lists[2][:]), COPY)
            else:
                nc.scalar.activation(b[:, : J // 2], g1[r][:].indirect(column_lists[1][:, : J // 32]), COPY)
                nc.vector.tensor_copy(b[:, J // 2 :], g1[r][:].indirect(column_lists[1][:, J // 32 :]))
                nc.vector.tensor_copy(third[:], g1[r][:].indirect(column_lists[2][:]))
            nc.vector.tensor_scalar(bf[:, r, :], b[:], f, None, MULT)
            nc.vector.scalar_tensor_tensor(hi[:, r, :], a[:, r, :], f, bf[:, r, :], MULT, MAX)
            nc.vector.scalar_tensor_tensor(lo[:, r, :], a[:, r, :], f, bf[:, r, :], MULT, MIN)
            nc.vector.scalar_tensor_tensor(mid[:, r, :], third[:], f, hi[:, r, :], MULT, MIN)

        vals_woven = keep.tile([P, PACK, P * PACK], BF16, name="vals_woven", align_bytes=64)
        for t in range(PACK):
            picked = keep.tile([P, I], BF16, name=f"picked_vals{t}", tag=("b0", "third0", "b1", "third1")[t])
            nc.scalar.activation(picked[:], vals_raw[t][:].indirect(token_list[:]), COPY)
            pairs = picked[:].bitcast(F32)
            turned = psum.tile([P, 2, P], F32, name=f"turned{t}", tag="bank")
            for u in range(2):
                nc.tensor.transpose(turned[:, u, :], pairs[:, u : I // 2 : 2], identity[:])
            nc.scalar.copy(
                vals_woven[:, t, :].bitcast(F32).rearrange("p (e u) -> p e u", u=2),
                turned[:].rearrange("p u e -> p e u"),
            )

        gr1_operands = []
        for k in range(J // UNIT):
            cols = slice(k * UNIT, (k + 1) * UNIT)
            woven = keep.tile([P, UNIT, PACK], BF16, name=f"gr1_woven{k}", tag=f"unit_woven{k}", align_bytes=64)
            dst, lo_view = weave_views(woven[:], lo[:, :, cols])
            mid_view = weave_views(woven[:], mid[:, :, cols])[1]
            nc.vector.tensor_tensor(dst, lo_view, mid_view, MAX)
            codes = keep.tile([P, UNIT], U32, name=f"gr1_codes{k}", align_bytes=64)
            scales = keep.tile([P, UNIT], U8, name=f"gr1_scales{k}", align_bytes=64)
            nc.vector.quantize_mx(codes[:].bitcast(FP8X4), scales[:], woven[:].rearrange("p j r -> p (j r)"))
            gr1_operands.append((codes, scales))
            if k == 1:
                val_codes = keep.tile([P, E], U32, name="val_codes", tag="hi", align_bytes=64)
                val_scales = keep.tile([P, E], U8, name="val_scales", align_bytes=64)
                nc.vector.quantize_mx(
                    val_codes[:].bitcast(FP8X4), val_scales[:], vals_woven[:].rearrange("p t x -> p (t x)")
                )


        def product(k):
            jcols = slice(k * UNIT, (k + 1) * UNIT)
            codes, scales = gr1_operands[k]
            bank = psum.tile([P, PACK, UNIT], F32, name=f"out_bank{jcols.start}", tag="bank")
            for t in range(PACK):
                ecols = slice(t * P, (t + 1) * P)
                nc.tensor.matmul_mx(
                    bank[:, t, :],
                    lhsT=val_codes[:, ecols].bitcast(FP8X4),
                    lhsT_scale=val_scales[:, ecols],
                    rhs=codes[:].bitcast(FP8X4),
                    rhs_scale=scales[:],
                    start=True,
                    stop=True,
                )
            result = keep.tile([P, PACK, UNIT], F32, name=f"result{jcols.start}")
            nc.scalar.copy(result[:], bank[:])
            nc.sync.dma_start(out_rows[:, :, jcols], result[:])
            rounded = keep.tile([P, UNIT, PACK], BF16, name=f"rounded{jcols.start}", tag=f"unit_woven{J // UNIT - 1 - k}", align_bytes=64)
            dst, src = weave_views(rounded[:], result[:])
            nc.vector.tensor_copy(dst, src)
            nc.vector.quantize_mx(
                out_codes[:, jcols].bitcast(FP8X4), out_scales[:, jcols], rounded[:].rearrange("p j t -> p (j t)")
            )
            nc.sync.dma_start(code_rows[:, jcols], out_codes[:, jcols].bitcast(I32))

        for k in range(J // UNIT):
            product(k)

        for q in range(4):
            queue = nc.scalar if q % 2 else nc.sync
            queue.dma_start(
                out_2[0, 4 * q : 4 * q + 4, :].bitcast(I32), out_scales[32 * q : 32 * q + 4, :].bitcast(I32)
            )
